import numpy as np
import ml_dtypes


def mxq(x, axis, fmt="e4m3"):
    dtype, down = {"e4m3": (ml_dtypes.float8_e4m3fn, 7), "e5m2": (ml_dtypes.float8_e5m2, 14)}[fmt]
    v = np.moveaxis(np.asarray(x, np.float32).astype(ml_dtypes.bfloat16).astype(np.float64), axis, -1)
    blocks = v.reshape(v.shape[:-1] + (-1, 32))
    amax = np.abs(blocks).max(-1, keepdims=True)
    byte = np.maximum(np.where(amax > 0, np.frexp(amax)[1] - 1 + 127, 0) - down, 1)
    scale = np.exp2(byte - 127.0)
    codes = (blocks / scale).astype(np.float32).astype(dtype).astype(np.float64)
    return np.moveaxis((codes * scale).reshape(v.shape), -1, axis)


WIDE = False


def mx_kscale(k):
    if not WIDE:
        return np.ones(k)
    levels = np.array([10, -10, 5, -5, 0])
    if k % 512:
        return np.exp2(np.random.permutation(np.resize(levels, k // 32))).repeat(32)
    a = np.empty((k // 512, 16))
    for p in range(k // 512):
        a[p, :8] = np.random.permutation(np.resize(levels, 8))
        for g in range(8):
            far = levels[np.abs(levels - a[p, g]) >= 10]
            a[p, g + 8] = far[np.random.randint(len(far))]
    return np.exp2(a.ravel()).repeat(32)


BF16 = ml_dtypes.bfloat16


def bf(x):
    return np.asarray(x, np.float32).astype(BF16)


def f64(x):
    return np.asarray(x).astype(np.float64)

def planes(Y):
    n, m = Y.shape
    b = f64(bf(Y)).reshape(n // 32, 32, m)
    amax = np.abs(b).max(1)
    byte = np.clip(np.where(amax > 0, np.frexp(amax)[1] - 1 + 127 - 7, 1), 1, 254)
    codes = (b * np.exp2(127.0 - byte)[:, None, :]).reshape(n, m).astype(np.float32).astype(ml_dtypes.float8_e4m3fn).view(np.uint8)
    words = codes.reshape(n // 512, 128, 4, m).transpose(0, 1, 3, 2)
    return np.ascontiguousarray(words), np.ascontiguousarray(byte.astype(np.uint8).reshape(n // 512, 16, m))


B, H, L, K, N, G = 16, 8, 8, 1024, 2048, 16
KEEP = 0.8


def setup_inputs():
    s = mx_kscale(K)
    c = np.exp(0.8 * np.random.randn(N))
    x = np.random.randn(B, H, L, K) * s
    w = np.random.randn(K, N) / np.sqrt(K) * c / s[:, None]
    bias = 0.5 * np.random.randn(N) * c
    path_mask = (np.random.rand(B, G) < KEEP) / KEEP
    shortcut = np.random.randn(B, H, L, N) * c
    return {"x": bf(x), "w": bf(w), "bias": bf(bias),
            "path_mask": bf(path_mask), "shortcut": bf(shortcut)}


def reference(x, w, bias, path_mask, shortcut):
    xq = mxq(f64(x).reshape(B * H * L, K), 1, "e4m3")
    wq = mxq(f64(w), 0, "e4m3")
    h = (xq @ wq) + f64(bias)
    a = h * np.minimum(np.maximum(h + 3.0, 0.0), 6.0) / 6.0
    kept = a.reshape(B, H * L, G, N // G) * f64(path_mask)[:, None, :, None]
    y = f64(shortcut) + kept.reshape(B, H, L, N)
    Y = y.reshape(B * H * L, N).T
    words, scales = planes(Y)
    return y, words, scales

@@ -1,0 +1,321 @@
+from contextlib import ExitStack
+
+import concourse.mybir as mybir
+from concourse.masks import make_identity
+
+TOKENS, K, N = 1024, 1024, 2048
+FLOPS = 2 * TOKENS * K * N
+
+F32 = mybir.dt.float32
+BF16 = mybir.dt.bfloat16
+I32 = mybir.dt.int32
+U32 = mybir.dt.uint32
+U8 = mybir.dt.uint8
+FP8X4 = mybir.dt.float8_e4m3fn_x4
+ALU = mybir.AluOpType
+ACT = mybir.ActivationFunctionType
+
+P = 128
+PASSES = 2
+HALVES = 2
+SLOTS = 4
+HALF = 512
+CHUNK = 512
+CHUNKS = 4
+TILES = 16
+STEPS = 32
+UNITS = 8
+
+
+def tile_pointwise_hardswish_droppath_g1_kernel(
+    tc, x, w, bias, path_mask, shortcut, out_0, out_1, out_2
+):
+    nc = tc.nc
+    x_hbm = x.rearrange("b h l k -> (b h l) k").rearrange("(v p i) k -> v p i k", v=HALVES, i=SLOTS)
+    s_hbm = shortcut.rearrange("b h l c -> (b h l) c").rearrange("(v p i) c -> v p i c", v=HALVES, i=SLOTS)
+    y_hbm = out_0.rearrange("b h l c -> (b h l) c").rearrange("(v p i) c -> v p i c", v=HALVES, i=SLOTS)
+    w_hbm = w.rearrange("(g p t) c -> g p t c", g=PASSES, t=4)
+    words_hbm = out_1.rearrange("g p m t -> g p (m t)").bitcast(I32)
+    scales_hbm = out_2.bitcast(I32)
+
+    with ExitStack() as ctx:
+        keep = ctx.enter_context(tc.tile_pool(name="keep", bufs=1))
+        work = ctx.enter_context(tc.tile_pool(name="work", bufs=3))
+        psum = ctx.enter_context(tc.psum_pool(name="psum", bufs=2))
+        ctx.enter_context(tc.manual_schedule())
+
+        x_rows = {}
+        w_cols = {}
+        s_tiles = {}
+
+        def load_x(v, i0, count):
+            raw = keep.tile([P, count * K], BF16, name="x_raw_%d_%d" % (v, i0))
+            nc.sync.dma_start(out=raw[:].rearrange("p (i k) -> p i k", i=count), in_=x_hbm[v, :, i0 : i0 + count, :])
+            for i in range(count):
+                x_rows[(v, i0 + i)] = raw[:].bitcast(F32)[:, i * (K // 2) : (i + 1) * (K // 2)]
+
+        def load_w(g, j0, count):
+            raw = keep.tile([P, 4, count * P], BF16, name="w_raw_%d_%d" % (g, j0))
+            nc.sync.dma_start(out=raw[:], in_=w_hbm[g, :, :, j0 * P : (j0 + count) * P])
+            for j in range(count):
+                w_cols[(j0 + j, g)] = raw[:, :, j * P : (j + 1) * P]
+
+        def load_s(v, c0):
+            raw = keep.tile([P, SLOTS, 2 * CHUNK], BF16, name="s_raw_%d_%d" % (v, c0))
+            nc.sync.dma_start(out=raw[:], in_=s_hbm[v, :, :, c0 * CHUNK : (c0 + 2) * CHUNK])
+            for j in range(8):
+                s_tiles[(v, 4 * c0 + j)] = raw[:, :, j * P : (j + 1) * P]
+
+        bias_rows = keep.tile([TILES, P], BF16)
+        mask_cols = keep.tile([P, HALVES * TILES], BF16)
+        nc.sync.dma_start(out=bias_rows[:], in_=bias.rearrange("(j p) -> j p", p=P))
+        load_x(0, 0, 1)
+        load_w(0, 0, 2)
+        load_w(1, 0, 2)
+        load_x(0, 1, 1)
+        load_x(0, 2, 1)
+        load_x(0, 3, 1)
+        load_w(0, 2, 2)
+        load_w(1, 2, 2)
+        load_x(1, 0, 2)
+        load_x(1, 2, 2)
+        for v in range(HALVES):
+            nc.sync.dma_start(
+                out=mask_cols[:, v * TILES : (v + 1) * TILES],
+                in_=path_mask[8 * v : 8 * v + 8, :].unsqueeze(1).to_broadcast([8, 16, TILES]),
+            )
+        load_w(0, 4, 4)
+        load_w(1, 4, 4)
+        load_s(0, 0)
+        load_s(1, 0)
+        load_w(0, 8, 8)
+        load_w(1, 8, 8)
+        load_s(0, 2)
+        load_s(1, 2)
+
+        ident = keep.tile([P, P], F32)
+        make_identity(nc, ident[:])
+
+        bias_f32 = keep.tile([P, P], F32)
+        nc.vector.memset(bias_f32[:], 0.0)
+        nc.vector.tensor_copy(out=bias_f32[:TILES, :], in_=bias_rows[:])
+        bias_bank = psum.tile([P, P], F32, tag="acc", bufs=4)
+        nc.tensor.transpose(bias_bank[:], bias_f32[:], ident[:])
+        gate_bias = keep.tile([P, TILES], F32)
+        bias_col = keep.tile([P, TILES], F32)
+        nc.scalar.activation(out=gate_bias[:], in_=bias_bank[:, :TILES], func=ACT.Identity, scale=1.0 / 6.0, bias=0.5)
+        nc.scalar.copy(out=bias_col[:], in_=bias_bank[:, :TILES])
+
+        x_codes = keep.tile([P, HALVES * PASSES * HALF], U32, align_bytes=64)
+        x_scales = keep.tile([P, HALVES * PASSES * HALF], U8, align_bytes=64)
+        y_scales = keep.tile([P, TOKENS], U8, align_bytes=64)
+        x_banks, x_grouped = {}, {}
+        w_grouped, w_codes, w_scales = {}, {}, {}
+        acc, gate_in, gate, act, act_bank = {}, {}, {}, {}, {}
+        y_tile, y_pairs, pair_bank, y_grouped = {}, {}, {}, {}
+
+        def x_transpose(v, i, tag):
+            bank = psum.tile([P, PASSES, 2, P], F32, tag=tag, name="x_bank")
+            for g in range(PASSES):
+                for u in range(2):
+                    nc.tensor.transpose(bank[:, g, u, :], x_rows[(v, i)][:, 256 * g + u : 256 * (g + 1) : 2], ident[:])
+            x_banks[(v, i)] = bank
+
+        def x_copy(v, i):
+            grouped = work.tile([P, PASSES * HALF], BF16, tag="x_grouped", bufs=4, align_bytes=64, name="x_grouped")
+            nc.scalar.copy(
+                out=grouped[:].bitcast(F32).rearrange("q (g p u) -> q g p u", g=PASSES, u=2),
+                in_=x_banks[(v, i)][:].rearrange("q g u p -> q g p u"),
+            )
+            x_grouped[(v, i)] = grouped
+
+        def x_quantize(v, i):
+            for g in range(PASSES):
+                c0 = (v * PASSES + g) * HALF + i * P
+                nc.vector.quantize_mx(
+                    out=x_codes[:, c0 : c0 + P].bitcast(FP8X4),
+                    scales=x_scales[:, c0 : c0 + P],
+                    in_=x_grouped[(v, i)][:, g * HALF : (g + 1) * HALF],
+                )
+
+        def w_group_tile(j):
+            w_grouped[j] = work.tile([P, PASSES * 4 * P], BF16, tag="w_grouped", align_bytes=64, name="w_grouped")
+
+        def w_interleave_vector(j, g):
+            if g == 0:
+                w_group_tile(j)
+            nc.vector.tensor_copy(
+                out=w_grouped[j][:, g * 4 * P : (g + 1) * 4 * P].rearrange("p (c i t) -> p c t i", i=4, t=4),
+                in_=w_cols[(j, g)].rearrange("p t (c i) -> p c t i", i=4),
+            )
+
+        def w_interleave_pool(j, g):
+            if g == 0:
+                w_group_tile(j)
+            nc.gpsimd.tensor_scalar(
+                out=w_grouped[j][:, g * 4 * P : (g + 1) * 4 * P].rearrange("p (n t) -> p n t", t=4),
+                in0=w_cols[(j, g)].rearrange("p t n -> p n t"),
+                scalar1=1.0,
+                scalar2=0.0,
+                op0=ALU.mult,
+                op1=ALU.add,
+            )
+
+        def w_quantize(j):
+            w_codes[j] = keep.tile([P, PASSES * P], U32, align_bytes=64, name="w_codes_%d" % j)
+            w_scales[j] = keep.tile([P, PASSES * P], U8, align_bytes=64, name="w_scales_%d" % j)
+            nc.vector.quantize_mx(out=w_codes[j][:].bitcast(FP8X4), scales=w_scales[j][:], in_=w_grouped[j][:])
+
+        def place(n):
+            c, v, jj = n // 8, (n // 4) % 2, n % 4
+            return v, 4 * c + jj
+
+        def multiply(n):
+            v, j = place(n)
+            acc[n] = psum.tile([P, HALF], F32, tag="acc", bufs=4, name="acc")
+            for g in range(PASSES):
+                c0 = (v * PASSES + g) * HALF
+                nc.tensor.matmul_mx(
+                    out=acc[n][:],
+                    lhsT=w_codes[j][:, g * P : (g + 1) * P].bitcast(FP8X4),
+                    lhsT_scale=w_scales[j][:, g * P : (g + 1) * P],
+                    rhs=x_codes[:, c0 : c0 + HALF].bitcast(FP8X4),
+                    rhs_scale=x_scales[:, c0 : c0 + HALF],
+                    start=(g == 0),
+                    stop=(g == PASSES - 1),
+                )
+
+        def gate_affine(n):
+            v, j = place(n)
+            gate_in[n] = work.tile([P, HALF], F32, tag="gate_in", name="gate_in")
+            nc.scalar.activation(
+                out=gate_in[n][:], in_=acc[n][:], func=ACT.Identity, scale=1.0 / 6.0, bias=gate_bias[:, j : j + 1]
+            )
+
+        def gate_clamp(n):
+            gate[n] = work.tile([P, HALF], F32, tag="gate", name="gate")
+            nc.gpsimd.tensor_scalar(
+                out=gate[n][:], in0=gate_in[n][:], scalar1=1.0, scalar2=0.0, op0=ALU.min, op1=ALU.max
+            )
+
+        def hard_swish(n):
+            v, j = place(n)
+            act[n] = work.tile([P, HALF], F32, tag="act", name="act")
+            nc.vector.scalar_tensor_tensor(
+                out=act[n][:], in0=acc[n][:], scalar=bias_col[:, j : j + 1], in1=gate[n][:], op0=ALU.add, op1=ALU.mult
+            )
+
+        def act_transpose(n):
+            act_bank[n] = psum.tile([P, SLOTS, P], F32, tag="act_bank", name="act_bank")
+            for i in range(SLOTS):
+                nc.tensor.transpose(act_bank[n][:, i, :], act[n][:, i * P : (i + 1) * P], ident[:])
+
+        def add_shortcut(n):
+            v, j = place(n)
+            unit, jj = divmod(n, 4)
+            if jj == 0:
+                y_tile[unit] = work.tile([P, SLOTS, CHUNK], F32, tag="y", bufs=4, name="y")
+            nc.vector.scalar_tensor_tensor(
+                out=y_tile[unit][:, :, jj * P : (jj + 1) * P],
+                in0=act_bank[n][:],
+                scalar=mask_cols[:, v * TILES + j : v * TILES + j + 1],
+                in1=s_tiles[(v, j)],
+                op0=ALU.mult,
+                op1=ALU.add,
+            )
+            if jj == 3:
+                c = unit // 2
+                nc.sync.dma_start(out=y_hbm[v, :, :, c * CHUNK : (c + 1) * CHUNK], in_=y_tile[unit][:])
+
+        def y_round(unit, i):
+            h, ii = divmod(i, 2)
+            if ii == 0:
+                y_pairs[(unit, h)] = work.tile([P, 2 * CHUNK], BF16, tag="y_pairs", name="y_pairs")
+            nc.scalar.copy(
+                out=y_pairs[(unit, h)][:, ii * CHUNK : (ii + 1) * CHUNK].rearrange("p (u q e) -> p u q e", u=2, e=2),
+                in_=y_tile[unit][:, i, :].rearrange("p (q u e) -> p u q e", u=2, e=2),
+            )
+
+        def y_transpose(unit, h):
+            bank = psum.tile([P, 4, P], F32, tag="pair_bank", name="pair_bank")
+            pairs = y_pairs[(unit, h)][:].bitcast(F32)
+            for r in range(4):
+                nc.tensor.transpose(bank[:, r, :], pairs[:, r * P : (r + 1) * P], ident[:])
+            pair_bank[(unit, h)] = bank
+
+        def y_copy(unit, h):
+            if h == 0:
+                y_grouped[unit] = work.tile([P, 4 * HALF], BF16, tag="y_grouped", bufs=2, align_bytes=64, name="y_grouped")
+            nc.scalar.copy(
+                out=y_grouped[unit][:].bitcast(F32).rearrange("q (p h r) -> q p h r", h=2, r=4)[:, :, h, :],
+                in_=pair_bank[(unit, h)][:].rearrange("q r p -> q p r"),
+            )
+
+        def y_quantize(unit):
+            c, v = divmod(unit, 2)
+            codes = work.tile([P, HALF], U32, tag="y_codes", align_bytes=64, name="y_codes")
+            nc.vector.quantize_mx(
+                out=codes[:].bitcast(FP8X4),
+                scales=y_scales[4 * c : P, v * HALF : (v + 1) * HALF],
+                in_=y_grouped[unit][:],
+            )
+            nc.sync.dma_start(out=words_hbm[c, :, v * HALF : (v + 1) * HALF], in_=codes[:].bitcast(I32))
+
+        for i in range(SLOTS):
+            x_transpose(0, i, "pair_bank" if i < 2 else "act_bank")
+            x_copy(0, i)
+        w_interleave_vector(0, 0)
+        w_interleave_vector(0, 1)
+        x_quantize(0, 0)
+        w_quantize(0)
+        w_interleave_vector(1, 0)
+        w_interleave_vector(1, 1)
+        x_quantize(0, 1)
+        w_quantize(1)
+        x_quantize(0, 2)
+        x_quantize(0, 3)
+
+        for s in range(STEPS + 12):
+            if s < STEPS:
+                multiply(s)
+            if s < SLOTS:
+                x_transpose(1, s, "pair_bank")
+            if 0 <= s - 4 < STEPS:
+                act_transpose(s - 4)
+            if s >= 11 and (s - 11) % 2 == 0 and (s - 11) // 4 < UNITS:
+                y_transpose((s - 11) // 4, ((s - 11) % 4) // 2)
+
+            if 0 <= s - 1 < STEPS:
+                gate_affine(s - 1)
+            if s < SLOTS:
+                x_copy(1, s)
+            if s >= 9 and (s - 9) // 4 < UNITS:
+                y_round((s - 9) // 4, (s - 9) % 4)
+            if s >= 12 and (s - 12) % 2 == 0 and (s - 12) // 4 < UNITS:
+                y_copy((s - 12) // 4, ((s - 12) % 4) // 2)
+
+            if 0 <= s - 2 < STEPS:
+                gate_clamp(s - 2)
+            if 0 <= s - 2 < 24:
+                w_interleave_pool(4 + 4 * ((s - 2) // 8) + ((s - 2) % 8) // 2, (s - 2) % 2)
+
+            if s < 2:
+                w_interleave_vector(2 + s, 0)
+                w_interleave_vector(2 + s, 1)
+            if 0 <= s - 3 < STEPS:
+                hard_swish(s - 3)
+            if 1 <= s < 3:
+                w_quantize(1 + s)
+            if 0 <= s - 5 < STEPS:
+                add_shortcut(s - 5)
+            if s < SLOTS:
+                x_quantize(1, s)
+            if 0 <= s - 4 < 24 and s % 2 == 0:
+                w_quantize(4 + 4 * ((s - 4) // 8) + ((s - 4) % 8) // 2)
+            if s >= 15 and (s - 15) % 4 == 0 and (s - 15) // 4 < UNITS:
+                y_quantize((s - 15) // 4)
+
+        for q in range(4):
+            nc.sync.dma_start(
+                out=scales_hbm[:, 4 * q : 4 * q + 4, :], in_=y_scales[32 * q : 32 * q + 16, :].bitcast(I32)
+            )

@@ -25,6 +25,11 @@ CHUNKS = 4
 TILES = 16
 STEPS = 32
 UNITS = 8
+ORDER = [(0, 0), (1, 0), (0, 1), (1, 1), (2, 0), (2, 1), (3, 0), (3, 1)]
+WB = 1
+PIECES = {3: [(3, 0), (3, 1)], 8: [(4, 0), (5, 0), (4, 1)], 11: [(5, 1)], 15: [(6, 0)], 19: [(6, 1), (7, 0)], 23: [(7, 1)]}
+PAIR_Q = {5: 3, 12: 4, 16: 5, 20: 6, 24: 7}
+XT = {5: [0, 1], 6: [2, 3]}
 
 
 def tile_pointwise_hardswish_droppath_g1_kernel(
@@ -47,6 +52,7 @@ def tile_pointwise_hardswish_droppath_g1_kernel(
         x_rows = {}
         w_cols = {}
         s_tiles = {}
+        w_pairs = {}
 
         def load_x(v, i0, count):
             raw = keep.tile([P, count * K], BF16, name="x_raw_%d_%d" % (v, i0))
@@ -59,39 +65,47 @@ def tile_pointwise_hardswish_droppath_g1_kernel(
             nc.sync.dma_start(out=raw[:], in_=w_hbm[g, :, :, j0 * P : (j0 + count) * P])
             for j in range(count):
                 w_cols[(j0 + j, g)] = raw[:, :, j * P : (j + 1) * P]
+            for j in range(0, count, 2):
+                w_pairs[((j0 + j) // 2, g)] = raw[:, :, j * P : (j + 2) * P]
 
-        def load_s(v, c0):
-            raw = keep.tile([P, SLOTS, 2 * CHUNK], BF16, name="s_raw_%d_%d" % (v, c0))
-            nc.sync.dma_start(out=raw[:], in_=s_hbm[v, :, :, c0 * CHUNK : (c0 + 2) * CHUNK])
-            for j in range(8):
+        def load_s(v, c0, count):
+            raw = keep.tile([P, SLOTS, count * CHUNK], BF16, name="s_raw_%d_%d" % (v, c0))
+            nc.sync.dma_start(out=raw[:], in_=s_hbm[v, :, :, c0 * CHUNK : (c0 + count) * CHUNK])
+            for j in range(4 * count):
                 s_tiles[(v, 4 * c0 + j)] = raw[:, :, j * P : (j + 1) * P]
 
         bias_rows = keep.tile([TILES, P], BF16)
         mask_cols = keep.tile([P, HALVES * TILES], BF16)
         nc.sync.dma_start(out=bias_rows[:], in_=bias.rearrange("(j p) -> j p", p=P))
         load_x(0, 0, 1)
-        load_w(0, 0, 2)
-        load_w(1, 0, 2)
         load_x(0, 1, 1)
         load_x(0, 2, 1)
         load_x(0, 3, 1)
+        load_w(0, 0, 2)
+        load_w(1, 0, 2)
         load_w(0, 2, 2)
         load_w(1, 2, 2)
-        load_x(1, 0, 2)
-        load_x(1, 2, 2)
+        load_w(0, 4, 2)
+        load_w(1, 4, 2)
+        load_w(0, 6, 2)
+        load_w(1, 6, 2)
         for v in range(HALVES):
             nc.sync.dma_start(
                 out=mask_cols[:, v * TILES : (v + 1) * TILES],
                 in_=path_mask[8 * v : 8 * v + 8, :].unsqueeze(1).to_broadcast([8, 16, TILES]),
             )
-        load_w(0, 4, 4)
-        load_w(1, 4, 4)
-        load_s(0, 0)
-        load_s(1, 0)
-        load_w(0, 8, 8)
-        load_w(1, 8, 8)
-        load_s(0, 2)
-        load_s(1, 2)
+        load_s(0, 0, 1)
+        load_x(1, 0, 2)
+        load_x(1, 2, 2)
+        load_w(0, 8, 4)
+        load_s(0, 1, 1)
+        load_w(1, 8, 4)
+        load_s(1, 0, 1)
+        load_w(0, 12, 4)
+        load_w(1, 12, 4)
+        load_s(1, 1, 1)
+        load_s(0, 2, 2)
+        load_s(1, 2, 2)
 
         ident = keep.tile([P, P], F32)
         make_identity(nc, ident[:])
@@ -103,14 +117,14 @@ def tile_pointwise_hardswish_droppath_g1_kernel(
         nc.tensor.transpose(bias_bank[:], bias_f32[:], ident[:])
         gate_bias = keep.tile([P, TILES], F32)
         bias_col = keep.tile([P, TILES], F32)
-        nc.scalar.activation(out=gate_bias[:], in_=bias_bank[:, :TILES], func=ACT.Identity, scale=1.0 / 6.0, bias=0.5)
+        nc.scalar.activation(out=gate_bias[:], in_=bias_bank[:, :TILES], func=ACT.Identity, scale=-1.0 / 6.0, bias=0.5)
         nc.scalar.copy(out=bias_col[:], in_=bias_bank[:, :TILES])
 
         x_codes = keep.tile([P, HALVES * PASSES * HALF], U32, align_bytes=64)
         x_scales = keep.tile([P, HALVES * PASSES * HALF], U8, align_bytes=64)
         y_scales = keep.tile([P, TOKENS], U8, align_bytes=64)
-        x_banks, x_grouped = {}, {}
-        w_grouped, w_codes, w_scales = {}, {}, {}
+        x_banks, x_grouped, x_sorted = {}, {}, {}
+        w_grouped, w_single, w_ops = {}, {}, {}
         acc, gate_in, gate, act, act_bank = {}, {}, {}, {}, {}
         y_tile, y_pairs, pair_bank, y_grouped = {}, {}, {}, {}
 
@@ -121,8 +135,23 @@ def tile_pointwise_hardswish_droppath_g1_kernel(
                     nc.tensor.transpose(bank[:, g, u, :], x_rows[(v, i)][:, 256 * g + u : 256 * (g + 1) : 2], ident[:])
             x_banks[(v, i)] = bank
 
+        def x_sort(i):
+            x_sorted[i] = work.tile([P, K // 2], F32, tag="x_sorted", bufs=4, name="x_sorted")
+            nc.vector.tensor_copy(
+                out=x_sorted[i][:].rearrange("p (g u q) -> p g u q", g=PASSES, u=2),
+                in_=x_rows[(0, i)].rearrange("p (g q u) -> p g u q", g=PASSES, u=2),
+            )
+
+        def x_transpose_sorted(i, tag):
+            bank = psum.tile([P, PASSES, 2, P], F32, tag=tag, name="x_bank")
+            for g in range(PASSES):
+                for u in range(2):
+                    r = 2 * g + u
+                    nc.tensor.transpose(bank[:, g, u, :], x_sorted[i][:, r * P : (r + 1) * P], ident[:])
+            x_banks[(0, i)] = bank
+
         def x_copy(v, i):
-            grouped = work.tile([P, PASSES * HALF], BF16, tag="x_grouped", bufs=4, align_bytes=64, name="x_grouped")
+            grouped = work.tile([P, PASSES * HALF], BF16, tag={(1, 1): "grouped", (1, 3): "grouped_b"}.get((v, i), "x_grouped"), bufs=1 if (v, i) in ((1, 1), (1, 3)) else 4, align_bytes=64, name="x_grouped")
             nc.scalar.copy(
                 out=grouped[:].bitcast(F32).rearrange("q (g p u) -> q g p u", g=PASSES, u=2),
                 in_=x_banks[(v, i)][:].rearrange("q g u p -> q g p u"),
@@ -139,36 +168,55 @@ def tile_pointwise_hardswish_droppath_g1_kernel(
                 )
 
         def w_group_tile(j):
-            w_grouped[j] = work.tile([P, PASSES * 4 * P], BF16, tag="w_grouped", align_bytes=64, name="w_grouped")
+            w_single[j] = work.tile([P, PASSES * 4 * P], BF16, tag="grouped" if j == 5 else "w_grouped", bufs=WB if j == 5 else 4, align_bytes=64, name="w_grouped")
 
         def w_interleave_vector(j, g):
             if g == 0:
                 w_group_tile(j)
             nc.vector.tensor_copy(
-                out=w_grouped[j][:, g * 4 * P : (g + 1) * 4 * P].rearrange("p (c i t) -> p c t i", i=4, t=4),
+                out=w_single[j][:, g * 4 * P : (g + 1) * 4 * P].rearrange("p (c i t) -> p c t i", i=4, t=4),
                 in_=w_cols[(j, g)].rearrange("p t (c i) -> p c t i", i=4),
             )
 
-        def w_interleave_pool(j, g):
+        def w_interleave_scalar(j, g):
             if g == 0:
                 w_group_tile(j)
+            nc.scalar.copy(
+                out=w_single[j][:, g * 4 * P : (g + 1) * 4 * P].rearrange("p (c i t) -> p c t i", i=4, t=4),
+                in_=w_cols[(j, g)].rearrange("p t (c i) -> p c t i", i=4),
+            )
+
+        def w_pair_interleave(pair, g):
+            if g == 0:
+                w_grouped[pair] = work.tile([P, PASSES * 8 * P], BF16, tag="grouped_b" if pair in (5, 7) else "grouped", bufs=1, align_bytes=64, name="w_pair")
             nc.gpsimd.tensor_scalar(
-                out=w_grouped[j][:, g * 4 * P : (g + 1) * 4 * P].rearrange("p (n t) -> p n t", t=4),
-                in0=w_cols[(j, g)].rearrange("p t n -> p n t"),
+                out=w_grouped[pair][:, g * 8 * P : (g + 1) * 8 * P].rearrange("p (n t) -> p n t", t=4),
+                in0=w_pairs[(pair, g)].rearrange("p t n -> p n t"),
                 scalar1=1.0,
                 scalar2=0.0,
                 op0=ALU.mult,
                 op1=ALU.add,
             )
 
+        def w_pair_quantize(pair):
+            codes = keep.tile([P, PASSES * 2 * P], U32, align_bytes=64, name="w_pair_codes_%d" % pair)
+            scales = keep.tile([P, PASSES * 2 * P], U8, align_bytes=64, name="w_pair_scales_%d" % pair)
+            nc.vector.quantize_mx(out=codes[:].bitcast(FP8X4), scales=scales[:], in_=w_grouped[pair][:])
+            for jj in range(2):
+                for g in range(PASSES):
+                    cols = slice((2 * g + jj) * P, (2 * g + jj + 1) * P)
+                    w_ops[(2 * pair + jj, g)] = (codes[:, cols], scales[:, cols])
+
         def w_quantize(j):
-            w_codes[j] = keep.tile([P, PASSES * P], U32, align_bytes=64, name="w_codes_%d" % j)
-            w_scales[j] = keep.tile([P, PASSES * P], U8, align_bytes=64, name="w_scales_%d" % j)
-            nc.vector.quantize_mx(out=w_codes[j][:].bitcast(FP8X4), scales=w_scales[j][:], in_=w_grouped[j][:])
+            codes = keep.tile([P, PASSES * P], U32, align_bytes=64, name="w_codes_%d" % j)
+            scales = keep.tile([P, PASSES * P], U8, align_bytes=64, name="w_scales_%d" % j)
+            nc.vector.quantize_mx(out=codes[:].bitcast(FP8X4), scales=scales[:], in_=w_single[j][:])
+            for g in range(PASSES):
+                w_ops[(j, g)] = (codes[:, g * P : (g + 1) * P], scales[:, g * P : (g + 1) * P])
 
         def place(n):
-            c, v, jj = n // 8, (n // 4) % 2, n % 4
-            return v, 4 * c + jj
+            c, v = ORDER[n // 4]
+            return v, 4 * c + n % 4
 
         def multiply(n):
             v, j = place(n)
@@ -177,8 +225,8 @@ def tile_pointwise_hardswish_droppath_g1_kernel(
                 c0 = (v * PASSES + g) * HALF
                 nc.tensor.matmul_mx(
                     out=acc[n][:],
-                    lhsT=w_codes[j][:, g * P : (g + 1) * P].bitcast(FP8X4),
-                    lhsT_scale=w_scales[j][:, g * P : (g + 1) * P],
+                    lhsT=w_ops[(j, g)][0].bitcast(FP8X4),
+                    lhsT_scale=w_ops[(j, g)][1],
                     rhs=x_codes[:, c0 : c0 + HALF].bitcast(FP8X4),
                     rhs_scale=x_scales[:, c0 : c0 + HALF],
                     start=(g == 0),
@@ -189,14 +237,12 @@ def tile_pointwise_hardswish_droppath_g1_kernel(
             v, j = place(n)
             gate_in[n] = work.tile([P, HALF], F32, tag="gate_in", name="gate_in")
             nc.scalar.activation(
-                out=gate_in[n][:], in_=acc[n][:], func=ACT.Identity, scale=1.0 / 6.0, bias=gate_bias[:, j : j + 1]
+                out=gate_in[n][:], in_=acc[n][:], func=ACT.Relu, scale=-1.0 / 6.0, bias=gate_bias[:, j : j + 1]
             )
 
         def gate_clamp(n):
             gate[n] = work.tile([P, HALF], F32, tag="gate", name="gate")
-            nc.gpsimd.tensor_scalar(
-                out=gate[n][:], in0=gate_in[n][:], scalar1=1.0, scalar2=0.0, op0=ALU.min, op1=ALU.max
-            )
+            nc.scalar.activation(out=gate[n][:], in_=gate_in[n][:], func=ACT.Relu, scale=-1.0, bias=1.0)
 
         def hard_swish(n):
             v, j = place(n)
@@ -206,7 +252,10 @@ def tile_pointwise_hardswish_droppath_g1_kernel(
             )
 
         def act_transpose(n):
-            act_bank[n] = psum.tile([P, SLOTS, P], F32, tag="act_bank", name="act_bank")
+            if n < STEPS - 1:
+                act_bank[n] = psum.tile([P, SLOTS, P], F32, tag="act_bank", name="act_bank")
+            else:
+                act_bank[n] = psum.tile([P, SLOTS, P], F32, tag="acc", bufs=4, name="act_bank")
             for i in range(SLOTS):
                 nc.tensor.transpose(act_bank[n][:, i, :], act[n][:, i * P : (i + 1) * P], ident[:])
 
@@ -223,37 +272,61 @@ def tile_pointwise_hardswish_droppath_g1_kernel(
                 op0=ALU.mult,
                 op1=ALU.add,
             )
-            if jj == 3:
-                c = unit // 2
-                nc.sync.dma_start(out=y_hbm[v, :, :, c * CHUNK : (c + 1) * CHUNK], in_=y_tile[unit][:])
+            c0 = ORDER[unit][0] * CHUNK
+            if unit == UNITS - 1 and jj % 2 == 1:
+                cols = slice((jj - 1) * P, (jj + 1) * P)
+                nc.sync.dma_start(
+                    out=y_hbm[v, :, :, c0 + cols.start : c0 + cols.stop], in_=y_tile[unit][:, :, cols]
+                )
+            elif jj == 3:
+                nc.sync.dma_start(out=y_hbm[v, :, :, c0 : c0 + CHUNK], in_=y_tile[unit][:])
 
-        def y_round(unit, i):
-            h, ii = divmod(i, 2)
-            if ii == 0:
-                y_pairs[(unit, h)] = work.tile([P, 2 * CHUNK], BF16, tag="y_pairs", name="y_pairs")
-            nc.scalar.copy(
-                out=y_pairs[(unit, h)][:, ii * CHUNK : (ii + 1) * CHUNK].rearrange("p (u q e) -> p u q e", u=2, e=2),
-                in_=y_tile[unit][:, i, :].rearrange("p (q u e) -> p u q e", u=2, e=2),
+        def y_round(unit, h):
+            y_pairs[(unit, h)] = work.tile([P, 2 * CHUNK], BF16, tag="y_pairs", name="y_pairs")
+            nc.gpsimd.tensor_scalar(
+                out=y_pairs[(unit, h)][:].rearrange("p (u q e) -> p u q e", u=2, e=2),
+                in0=y_tile[unit][:, 2 * h : 2 * h + 2, :].rearrange("p i (q u e) -> p u (i q) e", u=2, e=2),
+                scalar1=1.0,
+                scalar2=1.0,
+                op0=ALU.mult,
+                op1=ALU.mult,
             )
 
+        def y_round_last(jj, copy):
+            unit = UNITS - 1
+            for h in range(2):
+                if jj == 0:
+                    y_pairs[(unit, h)] = work.tile([P, 2 * CHUNK], BF16, tag="y_pairs_last", name="y_pairs_last")
+                copy(
+                    out=y_pairs[(unit, h)][:].rearrange("p (u i q e) -> p u i q e", u=2, i=2, e=2)[
+                        :, :, :, 32 * jj : 32 * jj + 32, :
+                    ],
+                    in_=y_tile[unit][:, 2 * h : 2 * h + 2, jj * P : (jj + 1) * P].rearrange(
+                        "p i (q u e) -> p u i q e", u=2, e=2
+                    ),
+                )
+
         def y_transpose(unit, h):
-            bank = psum.tile([P, 4, P], F32, tag="pair_bank", name="pair_bank")
+            if unit < UNITS - 1:
+                bank = psum.tile([P, 4, P], F32, tag="pair_bank", name="pair_bank")
+            else:
+                bank = psum.tile([P, 4, P], F32, tag="acc", bufs=4, name="pair_bank")
             pairs = y_pairs[(unit, h)][:].bitcast(F32)
             for r in range(4):
                 nc.tensor.transpose(bank[:, r, :], pairs[:, r * P : (r + 1) * P], ident[:])
             pair_bank[(unit, h)] = bank
 
-        def y_copy(unit, h):
+        def y_copy(unit, h, copy):
             if h == 0:
-                y_grouped[unit] = work.tile([P, 4 * HALF], BF16, tag="y_grouped", bufs=2, align_bytes=64, name="y_grouped")
-            nc.scalar.copy(
-                out=y_grouped[unit][:].bitcast(F32).rearrange("q (p h r) -> q p h r", h=2, r=4)[:, :, h, :],
-                in_=pair_bank[(unit, h)][:].rearrange("q r p -> q p r"),
+                y_grouped[unit] = work.tile([P, 4 * HALF], BF16, tag="y_grouped", bufs=4, align_bytes=64, name="y_grouped")
+            copy(
+                out=y_grouped[unit][:].bitcast(F32).rearrange("q (p h i u) -> q p h i u", h=2, i=2, u=2)[:, :, h, :, :],
+                in_=pair_bank[(unit, h)][:].rearrange("q (u i) p -> q p i u", u=2),
             )
 
         def y_quantize(unit):
-            c, v = divmod(unit, 2)
-            codes = work.tile([P, HALF], U32, tag="y_codes", align_bytes=64, name="y_codes")
+            c, v = ORDER[unit]
+            codes = work.tile([P, HALF], U32, tag="y_codes", bufs=4, align_bytes=64, name="y_codes")
             nc.vector.quantize_mx(
                 out=codes[:].bitcast(FP8X4),
                 scales=y_scales[4 * c : P, v * HALF : (v + 1) * HALF],
@@ -261,61 +334,107 @@ def tile_pointwise_hardswish_droppath_g1_kernel(
             )
             nc.sync.dma_start(out=words_hbm[c, :, v * HALF : (v + 1) * HALF], in_=codes[:].bitcast(I32))
 
-        for i in range(SLOTS):
-            x_transpose(0, i, "pair_bank" if i < 2 else "act_bank")
+        def x_first(i):
+            x_transpose_sorted(i, "pair_bank" if i < 2 else "act_bank")
             x_copy(0, i)
-        w_interleave_vector(0, 0)
-        w_interleave_vector(0, 1)
-        x_quantize(0, 0)
-        w_quantize(0)
-        w_interleave_vector(1, 0)
-        w_interleave_vector(1, 1)
-        x_quantize(0, 1)
-        w_quantize(1)
-        x_quantize(0, 2)
-        x_quantize(0, 3)
 
-        for s in range(STEPS + 12):
+        x_sort(0)
+        x_first(0)
+        x_sort(1)
+        x_first(1)
+        x_sort(2)
+        x_first(2)
+        x_sort(3)
+        x_first(3)
+        x_quantize(0, 0)
+        w_interleave_vector(0, 0)
+        x_quantize(0, 1)
+        w_interleave_vector(0, 1)
+        x_quantize(0, 2)
+        w_quantize(0)
+        x_quantize(0, 3)
+        multiply(0)
+        w_interleave_scalar(1, 0)
+        w_interleave_scalar(1, 1)
+        w_interleave_vector(2, 0)
+        w_interleave_vector(2, 1)
+        w_quantize(1)
+        multiply(1)
+        w_interleave_scalar(3, 0)
+        w_interleave_scalar(3, 1)
+        gate_affine(0)
+        w_quantize(2)
+        multiply(2)
+        w_interleave_vector(4, 0)
+        w_quantize(3)
+        w_interleave_vector(4, 1)
+        w_interleave_vector(5, 0)
+        w_quantize(4)
+        w_interleave_vector(5, 1)
+        w_quantize(5)
+        gate_affine(1)
+        gate_clamp(0)
+
+        last = UNITS - 1
+        for s in range(3, STEPS + 5):
             if s < STEPS:
                 multiply(s)
-            if s < SLOTS:
-                x_transpose(1, s, "pair_bank")
             if 0 <= s - 4 < STEPS:
                 act_transpose(s - 4)
-            if s >= 11 and (s - 11) % 2 == 0 and (s - 11) // 4 < UNITS:
-                y_transpose((s - 11) // 4, ((s - 11) % 4) // 2)
+            for unit in range(last):
+                for h in range(2):
+                    if s == min(4 * unit + 12, STEPS + 3) + h:
+                        y_transpose(unit, h)
 
-            if 0 <= s - 1 < STEPS:
+            if s - 1 < STEPS:
                 gate_affine(s - 1)
-            if s < SLOTS:
-                x_copy(1, s)
-            if s >= 9 and (s - 9) // 4 < UNITS:
-                y_round((s - 9) // 4, (s - 9) % 4)
-            if s >= 12 and (s - 12) % 2 == 0 and (s - 12) // 4 < UNITS:
-                y_copy((s - 12) // 4, ((s - 12) % 4) // 2)
-
-            if 0 <= s - 2 < STEPS:
+            for unit in range(last):
+                for h in range(2):
+                    if s == min(4 * unit + 13, STEPS + 4) + h and unit < last - 2:
+                        y_copy(unit, h, nc.scalar.copy)
+            if s - 2 < STEPS:
                 gate_clamp(s - 2)
-            if 0 <= s - 2 < 24:
-                w_interleave_pool(4 + 4 * ((s - 2) // 8) + ((s - 2) % 8) // 2, (s - 2) % 2)
+            for i in XT.get(s - 1, []):
+                x_copy(1, i)
+            if s == STEPS + 1:
+                y_copy(last - 2, 0, nc.scalar.copy)
+                y_copy(last - 2, 1, nc.scalar.copy)
+            if 0 <= s - 6 - 4 * last < 3:
+                y_round_last(s - 6 - 4 * last, nc.scalar.copy)
 
-            if s < 2:
-                w_interleave_vector(2 + s, 0)
-                w_interleave_vector(2 + s, 1)
-            if 0 <= s - 3 < STEPS:
+            for i in XT.get(s, []):
+                x_transpose(1, i, "pair_bank")
+            for unit in range(last):
+                for h in range(2):
+                    if s == 4 * unit + 9 + h:
+                        y_round(unit, h)
+            for pair, g in PIECES.get(s, []):
+                w_pair_interleave(pair, g)
+
+            if s - 3 < STEPS:
                 hard_swish(s - 3)
-            if 1 <= s < 3:
-                w_quantize(1 + s)
             if 0 <= s - 5 < STEPS:
                 add_shortcut(s - 5)
-            if s < SLOTS:
-                x_quantize(1, s)
-            if 0 <= s - 4 < 24 and s % 2 == 0:
-                w_quantize(4 + 4 * ((s - 4) // 8) + ((s - 4) % 8) // 2)
-            if s >= 15 and (s - 15) % 4 == 0 and (s - 15) // 4 < UNITS:
-                y_quantize((s - 15) // 4)
+            for i in XT.get(s - 1, []):
+                x_quantize(1, i)
+            if s in PAIR_Q:
+                w_pair_quantize(PAIR_Q[s])
+            for unit in range(last - 3):
+                if s == 4 * unit + 16:
+                    y_quantize(unit)
+
+        y_round_last(3, nc.vector.tensor_copy)
+        for h in range(2):
+            y_transpose(last, h)
+        y_copy(last - 1, 0, nc.scalar.copy)
+        y_copy(last - 1, 1, nc.scalar.copy)
+        for unit in range(last - 3, last):
+            y_quantize(unit)
+        y_copy(last, 0, nc.scalar.copy)
+        y_copy(last, 1, nc.vector.tensor_copy)
+        y_quantize(last)
 
         for q in range(4):
-            nc.sync.dma_start(
+            (nc.sync if q % 2 else nc.scalar).dma_start(
                 out=scales_hbm[:, 4 * q : 4 * q + 4, :], in_=y_scales[32 * q : 32 * q + 16, :].bitcast(I32)
             )

@@ -3,8 +3,8 @@ from contextlib import ExitStack
 import concourse.mybir as mybir
 from concourse.masks import make_identity
 
-TOKENS, K, N = 1024, 1024, 2048
-FLOPS = 2 * TOKENS * K * N
+PIXELS, K, N = 1024, 1024, 2048
+FLOPS = 2 * PIXELS * K * N
 
 F32 = mybir.dt.float32
 BF16 = mybir.dt.bfloat16
@@ -19,17 +19,15 @@ P = 128
 PASSES = 2
 HALVES = 2
 SLOTS = 4
-HALF = 512
-CHUNK = 512
-CHUNKS = 4
-TILES = 16
-STEPS = 32
-UNITS = 8
-ORDER = [(0, 0), (1, 0), (0, 1), (1, 1), (2, 0), (2, 1), (3, 0), (3, 1)]
-WB = 1
-PIECES = {3: [(3, 0), (3, 1)], 8: [(4, 0), (5, 0), (4, 1)], 11: [(5, 1)], 15: [(6, 0)], 19: [(6, 1), (7, 0)], 23: [(7, 1)]}
-PAIR_Q = {5: 3, 12: 4, 16: 5, 20: 6, 24: 7}
-XT = {5: [0, 1], 6: [2, 3]}
+HALF = P * SLOTS
+GROUP = 512
+TILES = N // P
+IMAGES = 16
+UNITS = [(0, 0), (1, 0), (0, 1), (1, 1), (2, 0), (2, 1), (3, 0), (3, 1)]
+LAST = len(UNITS) - 1
+STEPS = 4 * len(UNITS)
+MASK_ROW = 32
+LAST_PARTS = [(0, 2), (2, 1), (3, 1)]
 
 
 def tile_pointwise_hardswish_droppath_g1_kernel(
@@ -49,114 +47,108 @@ def tile_pointwise_hardswish_droppath_g1_kernel(
         psum = ctx.enter_context(tc.psum_pool(name="psum", bufs=2))
         ctx.enter_context(tc.manual_schedule())
 
-        x_rows = {}
-        w_cols = {}
-        s_tiles = {}
-        w_pairs = {}
+        x_pairs, w_raw, s_raw = {}, {}, {}
 
         def load_x(v, i0, count):
             raw = keep.tile([P, count * K], BF16, name="x_raw_%d_%d" % (v, i0))
             nc.sync.dma_start(out=raw[:].rearrange("p (i k) -> p i k", i=count), in_=x_hbm[v, :, i0 : i0 + count, :])
             for i in range(count):
-                x_rows[(v, i0 + i)] = raw[:].bitcast(F32)[:, i * (K // 2) : (i + 1) * (K // 2)]
+                x_pairs[(v, i0 + i)] = raw[:].bitcast(F32)[:, i * (K // 2) : (i + 1) * (K // 2)]
 
         def load_w(g, j0, count):
             raw = keep.tile([P, 4, count * P], BF16, name="w_raw_%d_%d" % (g, j0))
             nc.sync.dma_start(out=raw[:], in_=w_hbm[g, :, :, j0 * P : (j0 + count) * P])
             for j in range(count):
-                w_cols[(j0 + j, g)] = raw[:, :, j * P : (j + 1) * P]
-            for j in range(0, count, 2):
-                w_pairs[((j0 + j) // 2, g)] = raw[:, :, j * P : (j + 2) * P]
+                w_raw[(j0 + j, g)] = (raw, j * P)
 
         def load_s(v, c0, count):
-            raw = keep.tile([P, SLOTS, count * CHUNK], BF16, name="s_raw_%d_%d" % (v, c0))
-            nc.sync.dma_start(out=raw[:], in_=s_hbm[v, :, :, c0 * CHUNK : (c0 + count) * CHUNK])
+            raw = keep.tile([P, SLOTS, count * GROUP], BF16, name="s_raw_%d_%d" % (v, c0))
+            nc.sync.dma_start(out=raw[:], in_=s_hbm[v, :, :, c0 * GROUP : (c0 + count) * GROUP])
             for j in range(4 * count):
-                s_tiles[(v, 4 * c0 + j)] = raw[:, :, j * P : (j + 1) * P]
+                s_raw[(v, 4 * c0 + j)] = raw[:, :, j * P : (j + 1) * P]
 
-        bias_rows = keep.tile([TILES, P], BF16)
-        mask_cols = keep.tile([P, HALVES * TILES], BF16)
-        nc.sync.dma_start(out=bias_rows[:], in_=bias.rearrange("(j p) -> j p", p=P))
-        load_x(0, 0, 1)
-        load_x(0, 1, 1)
-        load_x(0, 2, 1)
-        load_x(0, 3, 1)
-        load_w(0, 0, 2)
-        load_w(1, 0, 2)
-        load_w(0, 2, 2)
-        load_w(1, 2, 2)
-        load_w(0, 4, 2)
-        load_w(1, 4, 2)
-        load_w(0, 6, 2)
-        load_w(1, 6, 2)
-        for v in range(HALVES):
-            nc.sync.dma_start(
-                out=mask_cols[:, v * TILES : (v + 1) * TILES],
-                in_=path_mask[8 * v : 8 * v + 8, :].unsqueeze(1).to_broadcast([8, 16, TILES]),
-            )
+        bias_raw = keep.tile([TILES, P], BF16)
+        mask_raw = keep.tile([MASK_ROW + IMAGES, TILES], BF16)
+        for i in range(SLOTS):
+            load_x(0, i, 1)
+        for g in range(PASSES):
+            load_w(g, 0, 2)
+        nc.sync.dma_start(out=bias_raw[:], in_=bias.rearrange("(j p) -> j p", p=P))
+        nc.sync.dma_start(out=mask_raw[MASK_ROW:, :], in_=path_mask)
+        for j0 in range(2, 8, 2):
+            for g in range(PASSES):
+                load_w(g, j0, 2)
         load_s(0, 0, 1)
         load_x(1, 0, 2)
         load_x(1, 2, 2)
         load_w(0, 8, 4)
         load_s(0, 1, 1)
         load_w(1, 8, 4)
-        load_s(1, 0, 1)
+        load_s(1, 0, 2)
         load_w(0, 12, 4)
         load_w(1, 12, 4)
-        load_s(1, 1, 1)
         load_s(0, 2, 2)
         load_s(1, 2, 2)
 
         ident = keep.tile([P, P], F32)
         make_identity(nc, ident[:])
 
-        bias_f32 = keep.tile([P, P], F32)
-        nc.vector.memset(bias_f32[:], 0.0)
-        nc.vector.tensor_copy(out=bias_f32[:TILES, :], in_=bias_rows[:])
-        bias_bank = psum.tile([P, P], F32, tag="acc", bufs=4)
-        nc.tensor.transpose(bias_bank[:], bias_f32[:], ident[:])
+        small = keep.tile([P, P], F32)
+        spread = keep.tile([P, HALVES * P], F32)
+        nc.vector.memset(small[:], 0.0)
+        nc.vector.memset(spread[:], 0.0)
         gate_bias = keep.tile([P, TILES], F32)
         bias_col = keep.tile([P, TILES], F32)
-        nc.scalar.activation(out=gate_bias[:], in_=bias_bank[:, :TILES], func=ACT.Identity, scale=-1.0 / 6.0, bias=0.5)
-        nc.scalar.copy(out=bias_col[:], in_=bias_bank[:, :TILES])
+        mask_col = keep.tile([P, HALVES, TILES], F32)
+
+        def bias_to_partitions():
+            nc.vector.tensor_copy(out=small[:TILES, :], in_=bias_raw[:])
+            nc.vector.tensor_copy(out=small[MASK_ROW : MASK_ROW + IMAGES, :TILES], in_=mask_raw[MASK_ROW:, :])
+            bank = psum.tile([P, P], F32, tag="acc", bufs=4, name="small_bank")
+            nc.tensor.transpose(bank[:], small[:], ident[:])
+            nc.scalar.activation(out=gate_bias[:], in_=bank[:, :TILES], func=ACT.Identity, scale=-1.0 / 6.0, bias=0.5)
+            nc.scalar.copy(out=bias_col[:], in_=bank[:, :TILES])
+            nc.scalar.copy(
+                out=spread[:TILES, :].rearrange("j (b r) -> j b r", b=IMAGES),
+                in_=bank[:TILES, MASK_ROW : MASK_ROW + IMAGES].unsqueeze(2).to_broadcast([TILES, IMAGES, 16]),
+            )
+
+        def mask_to_partitions():
+            bank = psum.tile([P, HALVES, P], F32, tag="pair_bank", name="mask_bank")
+            for v in range(HALVES):
+                nc.tensor.transpose(bank[:, v, :], spread[:, v * P : (v + 1) * P], ident[:])
+            nc.scalar.copy(out=mask_col[:], in_=bank[:, :, :TILES])
 
         x_codes = keep.tile([P, HALVES * PASSES * HALF], U32, align_bytes=64)
         x_scales = keep.tile([P, HALVES * PASSES * HALF], U8, align_bytes=64)
-        y_scales = keep.tile([P, TOKENS], U8, align_bytes=64)
-        x_banks, x_grouped, x_sorted = {}, {}, {}
-        w_grouped, w_single, w_ops = {}, {}, {}
-        acc, gate_in, gate, act, act_bank = {}, {}, {}, {}, {}
-        y_tile, y_pairs, pair_bank, y_grouped = {}, {}, {}, {}
+        x_bank, x_grouped = {}, {}
 
-        def x_transpose(v, i, tag):
-            bank = psum.tile([P, PASSES, 2, P], F32, tag=tag, name="x_bank")
-            for g in range(PASSES):
-                for u in range(2):
-                    nc.tensor.transpose(bank[:, g, u, :], x_rows[(v, i)][:, 256 * g + u : 256 * (g + 1) : 2], ident[:])
-            x_banks[(v, i)] = bank
-
-        def x_sort(i):
-            x_sorted[i] = work.tile([P, K // 2], F32, tag="x_sorted", bufs=4, name="x_sorted")
+        def x_sort_and_turn(i):
+            ordered = work.tile([P, K // 2], F32, tag="gate_in", name="x_sorted")
             nc.vector.tensor_copy(
-                out=x_sorted[i][:].rearrange("p (g u q) -> p g u q", g=PASSES, u=2),
-                in_=x_rows[(0, i)].rearrange("p (g q u) -> p g u q", g=PASSES, u=2),
+                out=ordered[:].rearrange("p (g u q) -> p g u q", g=PASSES, u=2),
+                in_=x_pairs[(0, i)].rearrange("p (g q u) -> p g u q", g=PASSES, u=2),
             )
+            x_bank[(0, i)] = psum.tile([P, 4, P], F32, tag="pair_bank" if i < 2 else "act_bank", name="x_bank")
+            for r in range(4):
+                nc.tensor.transpose(x_bank[(0, i)][:, r, :], ordered[:, r * P : (r + 1) * P], ident[:])
 
-        def x_transpose_sorted(i, tag):
-            bank = psum.tile([P, PASSES, 2, P], F32, tag=tag, name="x_bank")
+        def x_turn(i):
+            x_bank[(1, i)] = psum.tile([P, 4, P], F32, tag="pair_bank", name="x_bank")
             for g in range(PASSES):
                 for u in range(2):
-                    r = 2 * g + u
-                    nc.tensor.transpose(bank[:, g, u, :], x_sorted[i][:, r * P : (r + 1) * P], ident[:])
-            x_banks[(0, i)] = bank
+                    pairs = x_pairs[(1, i)][:, 2 * P * g + u : 2 * P * (g + 1) : 2]
+                    nc.tensor.transpose(x_bank[(1, i)][:, 2 * g + u, :], pairs, ident[:])
 
         def x_copy(v, i):
-            grouped = work.tile([P, PASSES * HALF], BF16, tag={(1, 1): "grouped", (1, 3): "grouped_b"}.get((v, i), "x_grouped"), bufs=1 if (v, i) in ((1, 1), (1, 3)) else 4, align_bytes=64, name="x_grouped")
-            nc.scalar.copy(
-                out=grouped[:].bitcast(F32).rearrange("q (g p u) -> q g p u", g=PASSES, u=2),
-                in_=x_banks[(v, i)][:].rearrange("q g u p -> q g p u"),
+            tag = {(1, 1): "pool_a", (1, 3): "pool_b"}.get((v, i), "x_grouped")
+            x_grouped[(v, i)] = work.tile(
+                [P, PASSES * HALF], BF16, tag=tag, bufs=4 if tag == "x_grouped" else 1, align_bytes=64, name="x_grouped"
             )
-            x_grouped[(v, i)] = grouped
+            nc.scalar.copy(
+                out=x_grouped[(v, i)][:].bitcast(F32).rearrange("q (g p u) -> q g p u", g=PASSES, u=2),
+                in_=x_bank[(v, i)][:].rearrange("q (g u) p -> q g p u", u=2),
+            )
 
         def x_quantize(v, i):
             for g in range(PASSES):
@@ -167,92 +159,87 @@ def tile_pointwise_hardswish_droppath_g1_kernel(
                     in_=x_grouped[(v, i)][:, g * HALF : (g + 1) * HALF],
                 )
 
-        def w_group_tile(j):
-            w_single[j] = work.tile([P, PASSES * 4 * P], BF16, tag="grouped" if j == 5 else "w_grouped", bufs=WB if j == 5 else 4, align_bytes=64, name="w_grouped")
+        w_grouped, w_operand = {}, {}
 
-        def w_interleave_vector(j, g):
+        def w_views(j0, count, g, tag):
             if g == 0:
-                w_group_tile(j)
-            nc.vector.tensor_copy(
-                out=w_single[j][:, g * 4 * P : (g + 1) * 4 * P].rearrange("p (c i t) -> p c t i", i=4, t=4),
-                in_=w_cols[(j, g)].rearrange("p t (c i) -> p c t i", i=4),
+                w_grouped[j0] = work.tile(
+                    [P, PASSES * count * 4 * P], BF16, tag=tag, bufs=4 if tag == "w_grouped" else 1, align_bytes=64,
+                    name="w_grouped",
+                )
+            raw, c0 = w_raw[(j0, g)]
+            width = count * P
+            return w_grouped[j0][:, g * 4 * width : (g + 1) * 4 * width], raw[:, :, c0 : c0 + width]
+
+        def w_interleave(copy, j0, count, g, tag="w_grouped"):
+            grouped, rows = w_views(j0, count, g, tag)
+            copy(
+                out=grouped.rearrange("p (c e t) -> p c t e", e=4, t=4), in_=rows.rearrange("p t (c e) -> p c t e", e=4)
             )
 
-        def w_interleave_scalar(j, g):
-            if g == 0:
-                w_group_tile(j)
-            nc.scalar.copy(
-                out=w_single[j][:, g * 4 * P : (g + 1) * 4 * P].rearrange("p (c i t) -> p c t i", i=4, t=4),
-                in_=w_cols[(j, g)].rearrange("p t (c i) -> p c t i", i=4),
-            )
-
-        def w_pair_interleave(pair, g):
-            if g == 0:
-                w_grouped[pair] = work.tile([P, PASSES * 8 * P], BF16, tag="grouped_b" if pair in (5, 7) else "grouped", bufs=1, align_bytes=64, name="w_pair")
+        def w_interleave_pool(j0, g, tag):
+            grouped, rows = w_views(j0, 2, g, tag)
             nc.gpsimd.tensor_scalar(
-                out=w_grouped[pair][:, g * 8 * P : (g + 1) * 8 * P].rearrange("p (n t) -> p n t", t=4),
-                in0=w_pairs[(pair, g)].rearrange("p t n -> p n t"),
+                out=grouped.rearrange("p (n t) -> p n t", t=4),
+                in0=rows.rearrange("p t n -> p n t"),
                 scalar1=1.0,
                 scalar2=0.0,
                 op0=ALU.mult,
                 op1=ALU.add,
             )
 
-        def w_pair_quantize(pair):
-            codes = keep.tile([P, PASSES * 2 * P], U32, align_bytes=64, name="w_pair_codes_%d" % pair)
-            scales = keep.tile([P, PASSES * 2 * P], U8, align_bytes=64, name="w_pair_scales_%d" % pair)
-            nc.vector.quantize_mx(out=codes[:].bitcast(FP8X4), scales=scales[:], in_=w_grouped[pair][:])
-            for jj in range(2):
-                for g in range(PASSES):
-                    cols = slice((2 * g + jj) * P, (2 * g + jj + 1) * P)
-                    w_ops[(2 * pair + jj, g)] = (codes[:, cols], scales[:, cols])
-
-        def w_quantize(j):
-            codes = keep.tile([P, PASSES * P], U32, align_bytes=64, name="w_codes_%d" % j)
-            scales = keep.tile([P, PASSES * P], U8, align_bytes=64, name="w_scales_%d" % j)
-            nc.vector.quantize_mx(out=codes[:].bitcast(FP8X4), scales=scales[:], in_=w_single[j][:])
+        def w_quantize(j0, count):
+            codes = keep.tile([P, PASSES * count * P], U32, align_bytes=64, name="w_codes_%d" % j0)
+            scales = keep.tile([P, PASSES * count * P], U8, align_bytes=64, name="w_scales_%d" % j0)
+            nc.vector.quantize_mx(out=codes[:].bitcast(FP8X4), scales=scales[:], in_=w_grouped[j0][:])
             for g in range(PASSES):
-                w_ops[(j, g)] = (codes[:, g * P : (g + 1) * P], scales[:, g * P : (g + 1) * P])
+                for j in range(count):
+                    cols = slice((g * count + j) * P, (g * count + j + 1) * P)
+                    w_operand[(j0 + j, g)] = (codes[:, cols], scales[:, cols])
+
+        acc, gate_in, gate, act, act_bank = {}, {}, {}, {}, {}
+        y_tile, y_pairs, pair_bank, y_grouped = {}, {}, {}, {}
+        y_scales = keep.tile([P, PIXELS], U8, align_bytes=64)
 
         def place(n):
-            c, v = ORDER[n // 4]
+            c, v = UNITS[n // 4]
             return v, 4 * c + n % 4
 
         def multiply(n):
             v, j = place(n)
             acc[n] = psum.tile([P, HALF], F32, tag="acc", bufs=4, name="acc")
             for g in range(PASSES):
-                c0 = (v * PASSES + g) * HALF
+                cols = slice((v * PASSES + g) * HALF, (v * PASSES + g + 1) * HALF)
                 nc.tensor.matmul_mx(
                     out=acc[n][:],
-                    lhsT=w_ops[(j, g)][0].bitcast(FP8X4),
-                    lhsT_scale=w_ops[(j, g)][1],
-                    rhs=x_codes[:, c0 : c0 + HALF].bitcast(FP8X4),
-                    rhs_scale=x_scales[:, c0 : c0 + HALF],
+                    lhsT=w_operand[(j, g)][0].bitcast(FP8X4),
+                    lhsT_scale=w_operand[(j, g)][1],
+                    rhs=x_codes[:, cols].bitcast(FP8X4),
+                    rhs_scale=x_scales[:, cols],
                     start=(g == 0),
                     stop=(g == PASSES - 1),
                 )
 
-        def gate_affine(n):
-            v, j = place(n)
+        def gate_upper(n):
+            j = place(n)[1]
             gate_in[n] = work.tile([P, HALF], F32, tag="gate_in", name="gate_in")
             nc.scalar.activation(
                 out=gate_in[n][:], in_=acc[n][:], func=ACT.Relu, scale=-1.0 / 6.0, bias=gate_bias[:, j : j + 1]
             )
 
-        def gate_clamp(n):
+        def gate_lower(n):
             gate[n] = work.tile([P, HALF], F32, tag="gate", name="gate")
             nc.scalar.activation(out=gate[n][:], in_=gate_in[n][:], func=ACT.Relu, scale=-1.0, bias=1.0)
 
         def hard_swish(n):
-            v, j = place(n)
+            j = place(n)[1]
             act[n] = work.tile([P, HALF], F32, tag="act", name="act")
             nc.vector.scalar_tensor_tensor(
                 out=act[n][:], in0=acc[n][:], scalar=bias_col[:, j : j + 1], in1=gate[n][:], op0=ALU.add, op1=ALU.mult
             )
 
-        def act_transpose(n):
-            if n < STEPS - 1:
+        def act_turn(n):
+            if n < STEPS - 2:
                 act_bank[n] = psum.tile([P, SLOTS, P], F32, tag="act_bank", name="act_bank")
             else:
                 act_bank[n] = psum.tile([P, SLOTS, P], F32, tag="acc", bufs=4, name="act_bank")
@@ -262,59 +249,55 @@ def tile_pointwise_hardswish_droppath_g1_kernel(
         def add_shortcut(n):
             v, j = place(n)
             unit, jj = divmod(n, 4)
-            if jj == 0:
-                y_tile[unit] = work.tile([P, SLOTS, CHUNK], F32, tag="y", bufs=4, name="y")
+            first, count = (0, 4) if unit < LAST else [part for part in LAST_PARTS if part[0] <= jj][-1]
+            if jj == first:
+                if unit < LAST:
+                    y_tile[(unit, first)] = work.tile([P, SLOTS, GROUP], F32, tag="y", bufs=4, name="y")
+                else:
+                    y_tile[(unit, first)] = keep.tile([P, SLOTS, count * P], F32, name="y_last_%d" % first)
+            y = y_tile[(unit, first)]
             nc.vector.scalar_tensor_tensor(
-                out=y_tile[unit][:, :, jj * P : (jj + 1) * P],
+                out=y[:, :, (jj - first) * P : (jj - first + 1) * P],
                 in0=act_bank[n][:],
-                scalar=mask_cols[:, v * TILES + j : v * TILES + j + 1],
-                in1=s_tiles[(v, j)],
+                scalar=mask_col[:, v, j : j + 1],
+                in1=s_raw[(v, j)],
                 op0=ALU.mult,
                 op1=ALU.add,
             )
-            c0 = ORDER[unit][0] * CHUNK
-            if unit == UNITS - 1 and jj % 2 == 1:
-                cols = slice((jj - 1) * P, (jj + 1) * P)
-                nc.sync.dma_start(
-                    out=y_hbm[v, :, :, c0 + cols.start : c0 + cols.stop], in_=y_tile[unit][:, :, cols]
-                )
-            elif jj == 3:
-                nc.sync.dma_start(out=y_hbm[v, :, :, c0 : c0 + CHUNK], in_=y_tile[unit][:])
+            if jj == first + count - 1:
+                nc.sync.dma_start(out=y_hbm[v, :, :, (j + 1 - count) * P : (j + 1) * P], in_=y[:])
 
         def y_round(unit, h):
-            y_pairs[(unit, h)] = work.tile([P, 2 * CHUNK], BF16, tag="y_pairs", name="y_pairs")
+            y_pairs[(unit, h)] = work.tile([P, 2 * GROUP], BF16, tag="y_pairs", name="y_pairs")
             nc.gpsimd.tensor_scalar(
                 out=y_pairs[(unit, h)][:].rearrange("p (u q e) -> p u q e", u=2, e=2),
-                in0=y_tile[unit][:, 2 * h : 2 * h + 2, :].rearrange("p i (q u e) -> p u (i q) e", u=2, e=2),
+                in0=y_tile[(unit, 0)][:, 2 * h : 2 * h + 2, :].rearrange("p i (q u e) -> p u (i q) e", u=2, e=2),
                 scalar1=1.0,
                 scalar2=1.0,
                 op0=ALU.mult,
                 op1=ALU.mult,
             )
 
-        def y_round_last(jj, copy):
-            unit = UNITS - 1
+        def y_round_last(part, copy):
+            first, count = LAST_PARTS[part]
             for h in range(2):
-                if jj == 0:
-                    y_pairs[(unit, h)] = work.tile([P, 2 * CHUNK], BF16, tag="y_pairs_last", name="y_pairs_last")
+                if first == 0:
+                    y_pairs[(LAST, h)] = keep.tile([P, 2 * GROUP], BF16, name="y_pairs_last_%d" % h)
                 copy(
-                    out=y_pairs[(unit, h)][:].rearrange("p (u i q e) -> p u i q e", u=2, i=2, e=2)[
-                        :, :, :, 32 * jj : 32 * jj + 32, :
+                    out=y_pairs[(LAST, h)][:].rearrange("p (u i q e) -> p u i q e", u=2, i=2, e=2)[
+                        :, :, :, 32 * first : 32 * (first + count), :
                     ],
-                    in_=y_tile[unit][:, 2 * h : 2 * h + 2, jj * P : (jj + 1) * P].rearrange(
-                        "p i (q u e) -> p u i q e", u=2, e=2
-                    ),
+                    in_=y_tile[(LAST, first)][:, 2 * h : 2 * h + 2, :].rearrange("p i (q u e) -> p u i q e", u=2, e=2),
                 )
 
-        def y_transpose(unit, h):
-            if unit < UNITS - 1:
-                bank = psum.tile([P, 4, P], F32, tag="pair_bank", name="pair_bank")
+        def y_turn(unit, h):
+            if unit < LAST:
+                pair_bank[(unit, h)] = psum.tile([P, 4, P], F32, tag="pair_bank", name="pair_bank")
             else:
-                bank = psum.tile([P, 4, P], F32, tag="acc", bufs=4, name="pair_bank")
+                pair_bank[(unit, h)] = psum.tile([P, 4, P], F32, tag="acc", bufs=4, name="pair_bank")
             pairs = y_pairs[(unit, h)][:].bitcast(F32)
             for r in range(4):
-                nc.tensor.transpose(bank[:, r, :], pairs[:, r * P : (r + 1) * P], ident[:])
-            pair_bank[(unit, h)] = bank
+                nc.tensor.transpose(pair_bank[(unit, h)][:, r, :], pairs[:, r * P : (r + 1) * P], ident[:])
 
         def y_copy(unit, h, copy):
             if h == 0:
@@ -325,7 +308,7 @@ def tile_pointwise_hardswish_droppath_g1_kernel(
             )
 
         def y_quantize(unit):
-            c, v = ORDER[unit]
+            c, v = UNITS[unit]
             codes = work.tile([P, HALF], U32, tag="y_codes", bufs=4, align_bytes=64, name="y_codes")
             nc.vector.quantize_mx(
                 out=codes[:].bitcast(FP8X4),
@@ -334,107 +317,111 @@ def tile_pointwise_hardswish_droppath_g1_kernel(
             )
             nc.sync.dma_start(out=words_hbm[c, :, v * HALF : (v + 1) * HALF], in_=codes[:].bitcast(I32))
 
-        def x_first(i):
-            x_transpose_sorted(i, "pair_bank" if i < 2 else "act_bank")
+        vector_copy, scalar_copy = nc.vector.tensor_copy, nc.scalar.copy
+        for i in range(SLOTS):
+            x_sort_and_turn(i)
             x_copy(0, i)
-
-        x_sort(0)
-        x_first(0)
-        x_sort(1)
-        x_first(1)
-        x_sort(2)
-        x_first(2)
-        x_sort(3)
-        x_first(3)
         x_quantize(0, 0)
-        w_interleave_vector(0, 0)
+        w_interleave(vector_copy, 0, 1, 0)
         x_quantize(0, 1)
-        w_interleave_vector(0, 1)
+        w_interleave(vector_copy, 0, 1, 1)
         x_quantize(0, 2)
-        w_quantize(0)
+        for g in range(PASSES):
+            w_interleave(scalar_copy, 1, 1, g)
+        bias_to_partitions()
+        w_quantize(0, 1)
         x_quantize(0, 3)
         multiply(0)
-        w_interleave_scalar(1, 0)
-        w_interleave_scalar(1, 1)
-        w_interleave_vector(2, 0)
-        w_interleave_vector(2, 1)
-        w_quantize(1)
+        for g in range(PASSES):
+            w_interleave(vector_copy, 2, 1, g)
+        w_quantize(1, 1)
         multiply(1)
-        w_interleave_scalar(3, 0)
-        w_interleave_scalar(3, 1)
-        gate_affine(0)
-        w_quantize(2)
+        for g in range(PASSES):
+            w_interleave(scalar_copy, 3, 1, g)
+        gate_upper(0)
+        w_quantize(2, 1)
         multiply(2)
-        w_interleave_vector(4, 0)
-        w_quantize(3)
-        w_interleave_vector(4, 1)
-        w_interleave_vector(5, 0)
-        w_quantize(4)
-        w_interleave_vector(5, 1)
-        w_quantize(5)
-        gate_affine(1)
-        gate_clamp(0)
+        w_interleave(vector_copy, 4, 1, 0)
+        w_quantize(3, 1)
+        w_interleave(vector_copy, 4, 1, 1)
+        w_interleave(vector_copy, 5, 1, 0, "pool_a")
+        w_quantize(4, 1)
+        w_interleave(vector_copy, 5, 1, 1, "pool_a")
+        w_quantize(5, 1)
+        gate_upper(1)
+        gate_lower(0)
+        mask_to_partitions()
 
-        last = UNITS - 1
         for s in range(3, STEPS + 5):
+            unit, phase = divmod(s, 4)
+
             if s < STEPS:
                 multiply(s)
             if 0 <= s - 4 < STEPS:
-                act_transpose(s - 4)
-            for unit in range(last):
-                for h in range(2):
-                    if s == min(4 * unit + 12, STEPS + 3) + h:
-                        y_transpose(unit, h)
+                act_turn(s - 4)
+            if phase < 2 and 0 <= unit - 3 < LAST - 1:
+                y_turn(unit - 3, phase)
+            if s >= STEPS + 3:
+                y_turn(LAST - 1, s - STEPS - 3)
 
             if s - 1 < STEPS:
-                gate_affine(s - 1)
-            for unit in range(last):
-                for h in range(2):
-                    if s == min(4 * unit + 13, STEPS + 4) + h and unit < last - 2:
-                        y_copy(unit, h, nc.scalar.copy)
+                gate_upper(s - 1)
+            if phase in (1, 2) and 0 <= unit - 3 < LAST - 2:
+                y_copy(unit - 3, phase - 1, scalar_copy)
             if s - 2 < STEPS:
-                gate_clamp(s - 2)
-            for i in XT.get(s - 1, []):
-                x_copy(1, i)
+                gate_lower(s - 2)
+            if s in (6, 7):
+                x_copy(1, 2 * (s - 6))
+                x_copy(1, 2 * (s - 6) + 1)
             if s == STEPS + 1:
-                y_copy(last - 2, 0, nc.scalar.copy)
-                y_copy(last - 2, 1, nc.scalar.copy)
-            if 0 <= s - 6 - 4 * last < 3:
-                y_round_last(s - 6 - 4 * last, nc.scalar.copy)
+                y_copy(LAST - 2, 0, scalar_copy)
+                y_copy(LAST - 2, 1, scalar_copy)
+            if s >= STEPS + 3:
+                y_round_last(s - STEPS - 3, scalar_copy)
 
-            for i in XT.get(s, []):
-                x_transpose(1, i, "pair_bank")
-            for unit in range(last):
-                for h in range(2):
-                    if s == 4 * unit + 9 + h:
-                        y_round(unit, h)
-            for pair, g in PIECES.get(s, []):
-                w_pair_interleave(pair, g)
+            if s in (5, 6):
+                x_turn(2 * (s - 5))
+                x_turn(2 * (s - 5) + 1)
 
-            if s - 3 < STEPS:
+            if phase in (1, 2) and 0 <= unit - 2 < LAST:
+                y_round(unit - 2, phase - 1)
+            if s in (3, 8):
+                for g in range(PASSES):
+                    w_interleave_pool(6 if s == 3 else 8, g, "pool_a")
+            if phase == 3 and 2 <= unit < 6:
+                w_interleave_pool(10 if unit < 4 else 14, unit % 2, "pool_b")
+
+            if s <= STEPS:
                 hard_swish(s - 3)
-            if 0 <= s - 5 < STEPS:
+            if s == STEPS + 1:
+                add_shortcut(STEPS - 4)
+                hard_swish(STEPS - 2)
+                hard_swish(STEPS - 1)
+            elif s >= 5:
                 add_shortcut(s - 5)
-            for i in XT.get(s - 1, []):
-                x_quantize(1, i)
-            if s in PAIR_Q:
-                w_pair_quantize(PAIR_Q[s])
-            for unit in range(last - 3):
-                if s == 4 * unit + 16:
-                    y_quantize(unit)
+            if s in (6, 7):
+                x_quantize(1, 2 * (s - 6))
+                x_quantize(1, 2 * (s - 6) + 1)
+            if s == 5:
+                w_quantize(6, 2)
+            if phase == 0 and 3 <= unit <= 6:
+                w_quantize(2 * unit + 2, 2)
+            if phase == 0 and 0 <= unit - 4 < LAST - 3:
+                y_quantize(unit - 4)
+            if phase == 0 and unit in (3, 4):
+                w_interleave(vector_copy, 12, 2, unit - 3, "vector_pair")
 
-        y_round_last(3, nc.vector.tensor_copy)
+        y_round_last(2, vector_copy)
         for h in range(2):
-            y_transpose(last, h)
-        y_copy(last - 1, 0, nc.scalar.copy)
-        y_copy(last - 1, 1, nc.scalar.copy)
-        for unit in range(last - 3, last):
+            y_turn(LAST, h)
+        for h in range(2):
+            y_copy(LAST - 1, h, scalar_copy)
+        for unit in range(LAST - 3, LAST):
             y_quantize(unit)
-        y_copy(last, 0, nc.scalar.copy)
-        y_copy(last, 1, nc.vector.tensor_copy)
-        y_quantize(last)
+        y_copy(LAST, 0, scalar_copy)
+        y_copy(LAST, 1, vector_copy)
+        y_quantize(LAST)
 
         for q in range(4):
-            (nc.sync if q % 2 else nc.scalar).dma_start(
-                out=scales_hbm[:, 4 * q : 4 * q + 4, :], in_=y_scales[32 * q : 32 * q + 16, :].bitcast(I32)
-            )
+            queue = nc.sync if q % 2 else nc.scalar
+            queue.dma_start(out=scales_hbm[:, 4 * q : 4 * q + 4, :], in_=y_scales[32 * q : 32 * q + 16, :].bitcast(I32))

from contextlib import ExitStack

import concourse.mybir as mybir
from concourse.masks import make_identity

PIXELS, K, N = 1024, 1024, 2048
FLOPS = 2 * PIXELS * K * N

F32 = mybir.dt.float32
BF16 = mybir.dt.bfloat16
I32 = mybir.dt.int32
U32 = mybir.dt.uint32
U8 = mybir.dt.uint8
FP8X4 = mybir.dt.float8_e4m3fn_x4
ALU = mybir.AluOpType
ACT = mybir.ActivationFunctionType

P = 128
PASSES = 2
HALVES = 2
SLOTS = 4
HALF = P * SLOTS
GROUP = 512
TILES = N // P
IMAGES = 16
UNITS = [(0, 0), (1, 0), (0, 1), (1, 1), (2, 0), (2, 1), (3, 0), (3, 1)]
LAST = len(UNITS) - 1
STEPS = 4 * len(UNITS)
MASK_ROW = 32
LAST_PARTS = [(0, 2), (2, 1), (3, 1)]


def tile_pointwise_hardswish_droppath_g1_kernel(
    tc, x, w, bias, path_mask, shortcut, out_0, out_1, out_2
):
    nc = tc.nc
    x_hbm = x.rearrange("b h l k -> (b h l) k").rearrange("(v p i) k -> v p i k", v=HALVES, i=SLOTS)
    s_hbm = shortcut.rearrange("b h l c -> (b h l) c").rearrange("(v p i) c -> v p i c", v=HALVES, i=SLOTS)
    y_hbm = out_0.rearrange("b h l c -> (b h l) c").rearrange("(v p i) c -> v p i c", v=HALVES, i=SLOTS)
    w_hbm = w.rearrange("(g p t) c -> g p t c", g=PASSES, t=4)
    words_hbm = out_1.rearrange("g p m t -> g p (m t)").bitcast(I32)
    scales_hbm = out_2.bitcast(I32)

    with ExitStack() as ctx:
        keep = ctx.enter_context(tc.tile_pool(name="keep", bufs=1))
        work = ctx.enter_context(tc.tile_pool(name="work", bufs=3))
        psum = ctx.enter_context(tc.psum_pool(name="psum", bufs=2))
        ctx.enter_context(tc.manual_schedule())

        x_pairs, w_raw, s_raw = {}, {}, {}

        def load_x(v, i0, count):
            raw = keep.tile([P, count * K], BF16, name="x_raw_%d_%d" % (v, i0))
            nc.sync.dma_start(out=raw[:].rearrange("p (i k) -> p i k", i=count), in_=x_hbm[v, :, i0 : i0 + count, :])
            for i in range(count):
                x_pairs[(v, i0 + i)] = raw[:].bitcast(F32)[:, i * (K // 2) : (i + 1) * (K // 2)]

        def load_w(g, j0, count):
            raw = keep.tile([P, 4, count * P], BF16, name="w_raw_%d_%d" % (g, j0))
            nc.sync.dma_start(out=raw[:], in_=w_hbm[g, :, :, j0 * P : (j0 + count) * P])
            for j in range(count):
                w_raw[(j0 + j, g)] = (raw, j * P)

        def load_s(v, c0, count):
            raw = keep.tile([P, SLOTS, count * GROUP], BF16, name="s_raw_%d_%d" % (v, c0))
            nc.sync.dma_start(out=raw[:], in_=s_hbm[v, :, :, c0 * GROUP : (c0 + count) * GROUP])
            for j in range(4 * count):
                s_raw[(v, 4 * c0 + j)] = raw[:, :, j * P : (j + 1) * P]

        bias_raw = keep.tile([TILES, P], BF16)
        mask_raw = keep.tile([MASK_ROW + IMAGES, TILES], BF16)
        for i in range(SLOTS):
            load_x(0, i, 1)
        for g in range(PASSES):
            load_w(g, 0, 2)
        nc.sync.dma_start(out=bias_raw[:], in_=bias.rearrange("(j p) -> j p", p=P))
        nc.sync.dma_start(out=mask_raw[MASK_ROW:, :], in_=path_mask)
        for j0 in range(2, 8, 2):
            for g in range(PASSES):
                load_w(g, j0, 2)
        load_s(0, 0, 1)
        load_x(1, 0, 2)
        load_x(1, 2, 2)
        load_w(0, 8, 4)
        load_s(0, 1, 1)
        load_w(1, 8, 4)
        load_s(1, 0, 2)
        load_w(0, 12, 4)
        load_w(1, 12, 4)
        load_s(0, 2, 2)
        load_s(1, 2, 2)

        ident = keep.tile([P, P], F32)
        make_identity(nc, ident[:])

        small = keep.tile([P, P], F32)
        spread = keep.tile([P, HALVES * P], F32)
        nc.vector.memset(small[:], 0.0)
        nc.vector.memset(spread[:], 0.0)
        gate_bias = keep.tile([P, TILES], F32)
        bias_col = keep.tile([P, TILES], F32)
        mask_col = keep.tile([P, HALVES, TILES], F32)

        def bias_to_partitions():
            nc.vector.tensor_copy(out=small[:TILES, :], in_=bias_raw[:])
            nc.vector.tensor_copy(out=small[MASK_ROW : MASK_ROW + IMAGES, :TILES], in_=mask_raw[MASK_ROW:, :])
            bank = psum.tile([P, P], F32, tag="acc", bufs=4, name="small_bank")
            nc.tensor.transpose(bank[:], small[:], ident[:])
            nc.scalar.activation(out=gate_bias[:], in_=bank[:, :TILES], func=ACT.Identity, scale=-1.0 / 6.0, bias=0.5)
            nc.scalar.copy(out=bias_col[:], in_=bank[:, :TILES])
            nc.scalar.copy(
                out=spread[:TILES, :].rearrange("j (b r) -> j b r", b=IMAGES),
                in_=bank[:TILES, MASK_ROW : MASK_ROW + IMAGES].unsqueeze(2).to_broadcast([TILES, IMAGES, 16]),
            )

        def mask_to_partitions():
            bank = psum.tile([P, HALVES, P], F32, tag="pair_bank", name="mask_bank")
            for v in range(HALVES):
                nc.tensor.transpose(bank[:, v, :], spread[:, v * P : (v + 1) * P], ident[:])
            nc.scalar.copy(out=mask_col[:], in_=bank[:, :, :TILES])

        x_codes = keep.tile([P, HALVES * PASSES * HALF], U32, align_bytes=64)
        x_scales = keep.tile([P, HALVES * PASSES * HALF], U8, align_bytes=64)
        x_bank, x_grouped = {}, {}

        def x_sort_and_turn(i):
            ordered = work.tile([P, K // 2], F32, tag="gate_in", name="x_sorted")
            nc.vector.tensor_copy(
                out=ordered[:].rearrange("p (g u q) -> p g u q", g=PASSES, u=2),
                in_=x_pairs[(0, i)].rearrange("p (g q u) -> p g u q", g=PASSES, u=2),
            )
            x_bank[(0, i)] = psum.tile([P, 4, P], F32, tag="pair_bank" if i < 2 else "act_bank", name="x_bank")
            for r in range(4):
                nc.tensor.transpose(x_bank[(0, i)][:, r, :], ordered[:, r * P : (r + 1) * P], ident[:])

        def x_turn(i):
            x_bank[(1, i)] = psum.tile([P, 4, P], F32, tag="pair_bank", name="x_bank")
            for g in range(PASSES):
                for u in range(2):
                    pairs = x_pairs[(1, i)][:, 2 * P * g + u : 2 * P * (g + 1) : 2]
                    nc.tensor.transpose(x_bank[(1, i)][:, 2 * g + u, :], pairs, ident[:])

        def x_copy(v, i):
            tag = {(1, 1): "pool_a", (1, 3): "pool_b"}.get((v, i), "x_grouped")
            x_grouped[(v, i)] = work.tile(
                [P, PASSES * HALF], BF16, tag=tag, bufs=4 if tag == "x_grouped" else 1, align_bytes=64, name="x_grouped"
            )
            nc.scalar.copy(
                out=x_grouped[(v, i)][:].bitcast(F32).rearrange("q (g p u) -> q g p u", g=PASSES, u=2),
                in_=x_bank[(v, i)][:].rearrange("q (g u) p -> q g p u", u=2),
            )

        def x_quantize(v, i):
            for g in range(PASSES):
                c0 = (v * PASSES + g) * HALF + i * P
                nc.vector.quantize_mx(
                    out=x_codes[:, c0 : c0 + P].bitcast(FP8X4),
                    scales=x_scales[:, c0 : c0 + P],
                    in_=x_grouped[(v, i)][:, g * HALF : (g + 1) * HALF],
                )

        w_grouped, w_operand = {}, {}

        def w_views(j0, count, g, tag):
            if g == 0:
                w_grouped[j0] = work.tile(
                    [P, PASSES * count * 4 * P], BF16, tag=tag, bufs=4 if tag == "w_grouped" else 1, align_bytes=64,
                    name="w_grouped",
                )
            raw, c0 = w_raw[(j0, g)]
            width = count * P
            return w_grouped[j0][:, g * 4 * width : (g + 1) * 4 * width], raw[:, :, c0 : c0 + width]

        def w_interleave(copy, j0, count, g, tag="w_grouped"):
            grouped, rows = w_views(j0, count, g, tag)
            copy(
                out=grouped.rearrange("p (c e t) -> p c t e", e=4, t=4), in_=rows.rearrange("p t (c e) -> p c t e", e=4)
            )

        def w_interleave_pool(j0, g, tag):
            grouped, rows = w_views(j0, 2, g, tag)
            nc.gpsimd.tensor_scalar(
                out=grouped.rearrange("p (n t) -> p n t", t=4),
                in0=rows.rearrange("p t n -> p n t"),
                scalar1=1.0,
                scalar2=0.0,
                op0=ALU.mult,
                op1=ALU.add,
            )

        def w_quantize(j0, count):
            codes = keep.tile([P, PASSES * count * P], U32, align_bytes=64, name="w_codes_%d" % j0)
            scales = keep.tile([P, PASSES * count * P], U8, align_bytes=64, name="w_scales_%d" % j0)
            nc.vector.quantize_mx(out=codes[:].bitcast(FP8X4), scales=scales[:], in_=w_grouped[j0][:])
            for g in range(PASSES):
                for j in range(count):
                    cols = slice((g * count + j) * P, (g * count + j + 1) * P)
                    w_operand[(j0 + j, g)] = (codes[:, cols], scales[:, cols])

        acc, gate_in, gate, act, act_bank = {}, {}, {}, {}, {}
        y_tile, y_pairs, pair_bank, y_grouped = {}, {}, {}, {}
        y_scales = keep.tile([P, PIXELS], U8, align_bytes=64)

        def place(n):
            c, v = UNITS[n // 4]
            return v, 4 * c + n % 4

        def multiply(n):
            v, j = place(n)
            acc[n] = psum.tile([P, HALF], F32, tag="acc", bufs=4, name="acc")
            for g in range(PASSES):
                cols = slice((v * PASSES + g) * HALF, (v * PASSES + g + 1) * HALF)
                nc.tensor.matmul_mx(
                    out=acc[n][:],
                    lhsT=w_operand[(j, g)][0].bitcast(FP8X4),
                    lhsT_scale=w_operand[(j, g)][1],
                    rhs=x_codes[:, cols].bitcast(FP8X4),
                    rhs_scale=x_scales[:, cols],
                    start=(g == 0),
                    stop=(g == PASSES - 1),
                )

        def gate_upper(n):
            j = place(n)[1]
            gate_in[n] = work.tile([P, HALF], F32, tag="gate_in", name="gate_in")
            nc.scalar.activation(
                out=gate_in[n][:], in_=acc[n][:], func=ACT.Relu, scale=-1.0 / 6.0, bias=gate_bias[:, j : j + 1]
            )

        def gate_lower(n):
            gate[n] = work.tile([P, HALF], F32, tag="gate", name="gate")
            nc.scalar.activation(out=gate[n][:], in_=gate_in[n][:], func=ACT.Relu, scale=-1.0, bias=1.0)

        def hard_swish(n):
            j = place(n)[1]
            act[n] = work.tile([P, HALF], F32, tag="act", name="act")
            nc.vector.scalar_tensor_tensor(
                out=act[n][:], in0=acc[n][:], scalar=bias_col[:, j : j + 1], in1=gate[n][:], op0=ALU.add, op1=ALU.mult
            )

        def act_turn(n):
            if n < STEPS - 2:
                act_bank[n] = psum.tile([P, SLOTS, P], F32, tag="act_bank", name="act_bank")
            else:
                act_bank[n] = psum.tile([P, SLOTS, P], F32, tag="acc", bufs=4, name="act_bank")
            for i in range(SLOTS):
                nc.tensor.transpose(act_bank[n][:, i, :], act[n][:, i * P : (i + 1) * P], ident[:])

        def add_shortcut(n):
            v, j = place(n)
            unit, jj = divmod(n, 4)
            first, count = (0, 4) if unit < LAST else [part for part in LAST_PARTS if part[0] <= jj][-1]
            if jj == first:
                if unit < LAST:
                    y_tile[(unit, first)] = work.tile([P, SLOTS, GROUP], F32, tag="y", bufs=4, name="y")
                else:
                    y_tile[(unit, first)] = keep.tile([P, SLOTS, count * P], F32, name="y_last_%d" % first)
            y = y_tile[(unit, first)]
            nc.vector.scalar_tensor_tensor(
                out=y[:, :, (jj - first) * P : (jj - first + 1) * P],
                in0=act_bank[n][:],
                scalar=mask_col[:, v, j : j + 1],
                in1=s_raw[(v, j)],
                op0=ALU.mult,
                op1=ALU.add,
            )
            if jj == first + count - 1:
                nc.sync.dma_start(out=y_hbm[v, :, :, (j + 1 - count) * P : (j + 1) * P], in_=y[:])

        def y_round(unit, h):
            y_pairs[(unit, h)] = work.tile([P, 2 * GROUP], BF16, tag="y_pairs", name="y_pairs")
            nc.gpsimd.tensor_scalar(
                out=y_pairs[(unit, h)][:].rearrange("p (u q e) -> p u q e", u=2, e=2),
                in0=y_tile[(unit, 0)][:, 2 * h : 2 * h + 2, :].rearrange("p i (q u e) -> p u (i q) e", u=2, e=2),
                scalar1=1.0,
                scalar2=1.0,
                op0=ALU.mult,
                op1=ALU.mult,
            )

        def y_round_last(part, copy):
            first, count = LAST_PARTS[part]
            for h in range(2):
                if first == 0:
                    y_pairs[(LAST, h)] = keep.tile([P, 2 * GROUP], BF16, name="y_pairs_last_%d" % h)
                copy(
                    out=y_pairs[(LAST, h)][:].rearrange("p (u i q e) -> p u i q e", u=2, i=2, e=2)[
                        :, :, :, 32 * first : 32 * (first + count), :
                    ],
                    in_=y_tile[(LAST, first)][:, 2 * h : 2 * h + 2, :].rearrange("p i (q u e) -> p u i q e", u=2, e=2),
                )

        def y_turn(unit, h):
            if unit < LAST:
                pair_bank[(unit, h)] = psum.tile([P, 4, P], F32, tag="pair_bank", name="pair_bank")
            else:
                pair_bank[(unit, h)] = psum.tile([P, 4, P], F32, tag="acc", bufs=4, name="pair_bank")
            pairs = y_pairs[(unit, h)][:].bitcast(F32)
            for r in range(4):
                nc.tensor.transpose(pair_bank[(unit, h)][:, r, :], pairs[:, r * P : (r + 1) * P], ident[:])

        def y_copy(unit, h, copy):
            if h == 0:
                y_grouped[unit] = work.tile([P, 4 * HALF], BF16, tag="y_grouped", bufs=4, align_bytes=64, name="y_grouped")
            copy(
                out=y_grouped[unit][:].bitcast(F32).rearrange("q (p h i u) -> q p h i u", h=2, i=2, u=2)[:, :, h, :, :],
                in_=pair_bank[(unit, h)][:].rearrange("q (u i) p -> q p i u", u=2),
            )

        def y_quantize(unit):
            c, v = UNITS[unit]
            codes = work.tile([P, HALF], U32, tag="y_codes", bufs=4, align_bytes=64, name="y_codes")
            nc.vector.quantize_mx(
                out=codes[:].bitcast(FP8X4),
                scales=y_scales[4 * c : P, v * HALF : (v + 1) * HALF],
                in_=y_grouped[unit][:],
            )
            nc.sync.dma_start(out=words_hbm[c, :, v * HALF : (v + 1) * HALF], in_=codes[:].bitcast(I32))

        vector_copy, scalar_copy = nc.vector.tensor_copy, nc.scalar.copy
        for i in range(SLOTS):
            x_sort_and_turn(i)
            x_copy(0, i)
        x_quantize(0, 0)
        w_interleave(vector_copy, 0, 1, 0)
        x_quantize(0, 1)
        w_interleave(vector_copy, 0, 1, 1)
        x_quantize(0, 2)
        for g in range(PASSES):
            w_interleave(scalar_copy, 1, 1, g)
        bias_to_partitions()
        w_quantize(0, 1)
        x_quantize(0, 3)
        multiply(0)
        for g in range(PASSES):
            w_interleave(vector_copy, 2, 1, g)
        w_quantize(1, 1)
        multiply(1)
        for g in range(PASSES):
            w_interleave(scalar_copy, 3, 1, g)
        gate_upper(0)
        w_quantize(2, 1)
        multiply(2)
        w_interleave(vector_copy, 4, 1, 0)
        w_quantize(3, 1)
        w_interleave(vector_copy, 4, 1, 1)
        w_interleave(vector_copy, 5, 1, 0, "pool_a")
        w_quantize(4, 1)
        w_interleave(vector_copy, 5, 1, 1, "pool_a")
        w_quantize(5, 1)
        gate_upper(1)
        gate_lower(0)
        mask_to_partitions()

        for s in range(3, STEPS + 5):
            unit, phase = divmod(s, 4)

            if s < STEPS:
                multiply(s)
            if 0 <= s - 4 < STEPS:
                act_turn(s - 4)
            if phase < 2 and 0 <= unit - 3 < LAST - 1:
                y_turn(unit - 3, phase)
            if s >= STEPS + 3:
                y_turn(LAST - 1, s - STEPS - 3)

            if s - 1 < STEPS:
                gate_upper(s - 1)
            if phase in (1, 2) and 0 <= unit - 3 < LAST - 2:
                y_copy(unit - 3, phase - 1, scalar_copy)
            if s - 2 < STEPS:
                gate_lower(s - 2)
            if s in (6, 7):
                x_copy(1, 2 * (s - 6))
                x_copy(1, 2 * (s - 6) + 1)
            if s == STEPS + 1:
                y_copy(LAST - 2, 0, scalar_copy)
                y_copy(LAST - 2, 1, scalar_copy)
            if s >= STEPS + 3:
                y_round_last(s - STEPS - 3, scalar_copy)

            if s in (5, 6):
                x_turn(2 * (s - 5))
                x_turn(2 * (s - 5) + 1)

            if phase in (1, 2) and 0 <= unit - 2 < LAST:
                y_round(unit - 2, phase - 1)
            if s in (3, 8):
                for g in range(PASSES):
                    w_interleave_pool(6 if s == 3 else 8, g, "pool_a")
            if phase == 3 and 2 <= unit < 6:
                w_interleave_pool(10 if unit < 4 else 14, unit % 2, "pool_b")

            if s <= STEPS:
                hard_swish(s - 3)
            if s == STEPS + 1:
                add_shortcut(STEPS - 4)
                hard_swish(STEPS - 2)
                hard_swish(STEPS - 1)
            elif s >= 5:
                add_shortcut(s - 5)
            if s in (6, 7):
                x_quantize(1, 2 * (s - 6))
                x_quantize(1, 2 * (s - 6) + 1)
            if s == 5:
                w_quantize(6, 2)
            if phase == 0 and 3 <= unit <= 6:
                w_quantize(2 * unit + 2, 2)
            if phase == 0 and 0 <= unit - 4 < LAST - 3:
                y_quantize(unit - 4)
            if phase == 0 and unit in (3, 4):
                w_interleave(vector_copy, 12, 2, unit - 3, "vector_pair")

        y_round_last(2, vector_copy)
        for h in range(2):
            y_turn(LAST, h)
        for h in range(2):
            y_copy(LAST - 1, h, scalar_copy)
        for unit in range(LAST - 3, LAST):
            y_quantize(unit)
        y_copy(LAST, 0, scalar_copy)
        y_copy(LAST, 1, vector_copy)
        y_quantize(LAST)

        for q in range(4):
            queue = nc.sync if q % 2 else nc.scalar
            queue.dma_start(out=scales_hbm[:, 4 * q : 4 * q + 4, :], in_=y_scales[32 * q : 32 * q + 16, :].bitcast(I32))
